import numpy as np
import ml_dtypes

BF16 = ml_dtypes.bfloat16


def bf(x):
    return np.asarray(x, np.float32).astype(BF16)


def f32(x):
    return np.asarray(x, np.float32)


def f64(x):
    return np.asarray(x).astype(np.float64)


def striped(idx):
    return np.tile(idx.reshape(-1, 16).T, (8, 1))


def rows(idx, k):
    return np.tile(idx, (k, 1))


def look(tab, idx):
    return np.take_along_axis(f64(tab), rows(idx, len(tab)), axis=1)


K, S, V, N, M = 256, 2048, 1536, 1536, 512


def setup_inputs():
    return {"tab": f32(np.random.standard_normal((2, K, S))), "w": bf(np.random.standard_normal((K, M)) / np.sqrt(K)), "b": f32(0.5 * np.random.standard_normal((M, 1))), "offs": striped(np.random.permutation(S)[:N])}


def reference(tab, w, b, offs):
    idx = offs[:16].T.reshape(-1)
    x = (look(tab[0], idx) - 0.125) * 1.5 / (1.0 + np.exp(-look(tab[1], idx)))
    return np.maximum(f64(w).T @ x + f64(b), 0.0)

@@ -1,0 +1,63 @@
+import concourse.mybir as mybir
+
+F32, BF16, U16 = mybir.dt.float32, mybir.dt.bfloat16, mybir.dt.uint16
+ALU = mybir.AluOpType
+ACT = mybir.ActivationFunctionType
+
+P = 128
+GROUP = 16
+PIECE = 512
+SHIFT, SCALE = 0.125, 1.5
+FLOPS = 2 * 256 * 512 * 1536
+
+
+def tile_lookup_gnorm_relu_kernel(tc, tab, w, b, offs, out):
+    nc = tc.nc
+    rows, places = tab.shape[1], tab.shape[2]
+    m_total, n_total = out.shape
+    row_blocks, m_blocks, pieces = rows // P, m_total // P, n_total // PIECE
+
+    out_by_block = out.rearrange("(p c) n -> p c n", c=m_blocks)
+
+    with (
+        tc.tile_pool(name="held", bufs=1) as held,
+        tc.tile_pool(name="work", bufs=row_blocks * pieces) as work,
+        tc.tile_pool(name="results", bufs=m_blocks * pieces) as results,
+        tc.psum_pool(name="psum", bufs=8) as psum,
+    ):
+        offsets = held.tile([P, n_total // GROUP], U16, name="offsets")
+        nc.sync.dma_start(offsets[:], offs)
+        values = [held.tile([P, places], F32, name=f"values{k}") for k in range(row_blocks)]
+        gates = [held.tile([P, places], F32, name=f"gates{k}") for k in range(row_blocks)]
+        weights = held.tile([P, row_blocks, m_total], BF16, name="weights")
+        bias = held.tile([P, m_blocks], F32, name="bias")
+        for k in range(row_blocks):
+            nc.sync.dma_start(values[k][:], tab[0, k * P:(k + 1) * P, :])
+            nc.sync.dma_start(gates[k][:], tab[1, k * P:(k + 1) * P, :])
+        nc.sync.dma_start(weights[:], w.rearrange("(k p) m -> p k m", p=P))
+        nc.sync.dma_start(bias[:], b.rearrange("(p c) o -> p (c o)", c=m_blocks))
+
+        x = {}
+        for k in range(row_blocks):
+            for j in range(pieces):
+                listed = offsets[:, j * PIECE // GROUP:(j + 1) * PIECE // GROUP]
+                normed = work.tile([P, PIECE], F32, name="normed")
+                gate = work.tile([P, PIECE], F32, name="gate")
+                x[k, j] = work.tile([P, PIECE], BF16, name="x")
+                nc.vector.tensor_scalar(normed[:], values[k][:].indirect(listed), SHIFT, SCALE,
+                                        ALU.subtract, ALU.mult)
+                nc.scalar.activation(gate[:], gates[k][:].indirect(listed), ACT.Sigmoid)
+                nc.vector.tensor_tensor(x[k, j][:], normed[:], gate[:], ALU.mult)
+
+        for j in range(pieces):
+            for c in range(m_blocks):
+                sums = psum.tile([P, PIECE], F32, name="sums")
+                for k in range(row_blocks):
+                    nc.tensor.matmul(sums[:], weights[:, k, c::m_blocks], x[k, j][:],
+                                     start=(k == 0), stop=(k == row_blocks - 1))
+                result = results.tile([P, PIECE], F32, name="result")
+                if c % 2 == 0:
+                    nc.scalar.activation(result[:], sums[:], ACT.Relu, bias=bias[:, c:c + 1])
+                else:
+                    nc.vector.tensor_scalar(result[:], sums[:], bias[:, c:c + 1], 0.0, ALU.add, ALU.max)
+                nc.sync.dma_start(out_by_block[:, c, j * PIECE:(j + 1) * PIECE], result[:])

@@ -6,7 +6,9 @@ ACT = mybir.ActivationFunctionType
 
 P = 128
 GROUP = 16
-PIECE = 512
+PIECE = 256
+PAIR = 2
+BANKS = 8
 SHIFT, SCALE = 0.125, 1.5
 FLOPS = 2 * 256 * 512 * 1536
 
@@ -15,49 +17,62 @@ def tile_lookup_gnorm_relu_kernel(tc, tab, w, b, offs, out):
     nc = tc.nc
     rows, places = tab.shape[1], tab.shape[2]
     m_total, n_total = out.shape
-    row_blocks, m_blocks, pieces = rows // P, m_total // P, n_total // PIECE
+    row_blocks, out_blocks, pieces = rows // P, m_total // P, n_total // PIECE
+    early_pieces = BANKS // out_blocks
 
-    out_by_block = out.rearrange("(p c) n -> p c n", c=m_blocks)
+    out_by_block = out.rearrange("(p c) n -> p c n", c=out_blocks)
 
     with (
         tc.tile_pool(name="held", bufs=1) as held,
-        tc.tile_pool(name="work", bufs=row_blocks * pieces) as work,
-        tc.tile_pool(name="results", bufs=m_blocks * pieces) as results,
-        tc.psum_pool(name="psum", bufs=8) as psum,
+        tc.psum_pool(name="psum", bufs=BANKS) as psum,
     ):
-        offsets = held.tile([P, n_total // GROUP], U16, name="offsets")
-        nc.sync.dma_start(offsets[:], offs)
-        values = [held.tile([P, places], F32, name=f"values{k}") for k in range(row_blocks)]
-        gates = [held.tile([P, places], F32, name=f"gates{k}") for k in range(row_blocks)]
-        weights = held.tile([P, row_blocks, m_total], BF16, name="weights")
-        bias = held.tile([P, m_blocks], F32, name="bias")
-        for k in range(row_blocks):
-            nc.sync.dma_start(values[k][:], tab[0, k * P:(k + 1) * P, :])
-            nc.sync.dma_start(gates[k][:], tab[1, k * P:(k + 1) * P, :])
-        nc.sync.dma_start(weights[:], w.rearrange("(k p) m -> p k m", p=P))
-        nc.sync.dma_start(bias[:], b.rearrange("(p c) o -> p (c o)", c=m_blocks))
+        warm_in = held.tile([P, 1], F32, name="warm_in")
+        warm_out = held.tile([P, 1], F32, name="warm_out")
+        nc.vector.memset(warm_in[:], 0.0)
+        nc.scalar.activation(warm_out[:], warm_in[:], ACT.Sigmoid)
 
-        x = {}
+        offsets = held.tile([P, n_total // GROUP], U16, name="offsets")
+        bias = held.tile([P, out_blocks], F32, name="bias")
+        nc.sync.dma_start(offsets[:], offs)
+        values, gates, weights = [], [], []
         for k in range(row_blocks):
-            for j in range(pieces):
+            block_rows = slice(k * P, (k + 1) * P)
+            gates.append(held.tile([P, places], F32, name=f"gates{k}"))
+            values.append(held.tile([P, places], F32, name=f"values{k}"))
+            weights.append(held.tile([P, m_total], BF16, name=f"weights{k}"))
+            nc.sync.dma_start(gates[k][:], tab[1, block_rows, :])
+            nc.sync.dma_start(values[k][:], tab[0, block_rows, :])
+            nc.sync.dma_start(weights[k][:], w[block_rows, :])
+        nc.sync.dma_start(bias[:], b.rearrange("(p c) o -> p (c o)", c=out_blocks))
+
+        x = [held.tile([P, n_total], BF16, name=f"x{k}") for k in range(row_blocks)]
+        for k in range(row_blocks):
+            for step in range(pieces):
+                j = (step + pieces // 2) % pieces if k == 0 else step
                 listed = offsets[:, j * PIECE // GROUP:(j + 1) * PIECE // GROUP]
-                normed = work.tile([P, PIECE], F32, name="normed")
-                gate = work.tile([P, PIECE], F32, name="gate")
-                x[k, j] = work.tile([P, PIECE], BF16, name="x")
+                gate = held.tile([P, PIECE], F32, name=f"gate{k}_{j}")
+                normed = held.tile([P, PIECE], F32, name=f"normed{k}_{j}")
+                nc.scalar.activation(gate[:], gates[k][:].indirect(listed), ACT.Sigmoid)
                 nc.vector.tensor_scalar(normed[:], values[k][:].indirect(listed), SHIFT, SCALE,
                                         ALU.subtract, ALU.mult)
-                nc.scalar.activation(gate[:], gates[k][:].indirect(listed), ACT.Sigmoid)
-                nc.vector.tensor_tensor(x[k, j][:], normed[:], gate[:], ALU.mult)
+                last = k == row_blocks - 1 and step == pieces - 1
+                multiplier = nc.vector if last else nc.gpsimd
+                multiplier.tensor_tensor(x[k][:, j * PIECE:(j + 1) * PIECE], normed[:], gate[:], ALU.mult)
 
         for j in range(pieces):
-            for c in range(m_blocks):
-                sums = psum.tile([P, PIECE], F32, name="sums")
-                for k in range(row_blocks):
-                    nc.tensor.matmul(sums[:], weights[:, k, c::m_blocks], x[k, j][:],
+            columns = slice(j * PIECE, (j + 1) * PIECE)
+            sums = [psum.tile([P, PIECE], F32, name="sums") for c in range(out_blocks)]
+            for k in range(row_blocks):
+                for c in range(out_blocks):
+                    nc.tensor.matmul(sums[c][:], weights[k][:, c::out_blocks], x[k][:, columns],
                                      start=(k == 0), stop=(k == row_blocks - 1))
-                result = results.tile([P, PIECE], F32, name="result")
-                if c % 2 == 0:
-                    nc.scalar.activation(result[:], sums[:], ACT.Relu, bias=bias[:, c:c + 1])
-                else:
-                    nc.vector.tensor_scalar(result[:], sums[:], bias[:, c:c + 1], 0.0, ALU.add, ALU.max)
-                nc.sync.dma_start(out_by_block[:, c, j * PIECE:(j + 1) * PIECE], result[:])
+            for first in range(0, out_blocks, PAIR):
+                result = held.tile([P, PAIR, PIECE], F32, name=f"result{j}_{first}")
+                for c in range(first, first + PAIR):
+                    if j >= early_pieces and c % 2 == 1:
+                        nc.vector.tensor_scalar(result[:, c - first, :], sums[c][:], bias[:, c:c + 1], 0.0,
+                                                ALU.add, ALU.max)
+                    else:
+                        nc.scalar.activation(result[:, c - first, :], sums[c][:], ACT.Relu,
+                                             bias=bias[:, c:c + 1])
+                nc.sync.dma_start(out_by_block[:, first:first + PAIR, columns], result[:])

@@ -7,8 +7,9 @@ ACT = mybir.ActivationFunctionType
 P = 128
 GROUP = 16
 PIECE = 256
-PAIR = 2
+BANK = 512
 BANKS = 8
+STORE_WIDTHS = (PIECE, PIECE, 4 * PIECE)
 SHIFT, SCALE = 0.125, 1.5
 FLOPS = 2 * 256 * 512 * 1536
 
@@ -18,7 +19,7 @@ def tile_lookup_gnorm_relu_kernel(tc, tab, w, b, offs, out):
     rows, places = tab.shape[1], tab.shape[2]
     m_total, n_total = out.shape
     row_blocks, out_blocks, pieces = rows // P, m_total // P, n_total // PIECE
-    early_pieces = BANKS // out_blocks
+    assert sum(STORE_WIDTHS) == n_total
 
     out_by_block = out.rearrange("(p c) n -> p c n", c=out_blocks)
 
@@ -55,24 +56,27 @@ def tile_lookup_gnorm_relu_kernel(tc, tab, w, b, offs, out):
                 nc.scalar.activation(gate[:], gates[k][:].indirect(listed), ACT.Sigmoid)
                 nc.vector.tensor_scalar(normed[:], values[k][:].indirect(listed), SHIFT, SCALE,
                                         ALU.subtract, ALU.mult)
-                last = k == row_blocks - 1 and step == pieces - 1
-                multiplier = nc.vector if last else nc.gpsimd
+                late = k == row_blocks - 1 and step >= pieces - 2
+                multiplier = nc.vector if late else nc.gpsimd
                 multiplier.tensor_tensor(x[k][:, j * PIECE:(j + 1) * PIECE], normed[:], gate[:], ALU.mult)
 
-        for j in range(pieces):
-            columns = slice(j * PIECE, (j + 1) * PIECE)
-            sums = [psum.tile([P, PIECE], F32, name="sums") for c in range(out_blocks)]
-            for k in range(row_blocks):
-                for c in range(out_blocks):
-                    nc.tensor.matmul(sums[c][:], weights[k][:, c::out_blocks], x[k][:, columns],
-                                     start=(k == 0), stop=(k == row_blocks - 1))
-            for first in range(0, out_blocks, PAIR):
-                result = held.tile([P, PAIR, PIECE], F32, name=f"result{j}_{first}")
-                for c in range(first, first + PAIR):
-                    if j >= early_pieces and c % 2 == 1:
-                        nc.vector.tensor_scalar(result[:, c - first, :], sums[c][:], bias[:, c:c + 1], 0.0,
-                                                ALU.add, ALU.max)
+        start = 0
+        for width in STORE_WIDTHS:
+            for c in range(out_blocks):
+                result = held.tile([P, width], F32, name=f"result{start}_{c}")
+                part_width = min(width, BANK)
+                parts = range(0, width, part_width)
+                sums = [psum.tile([P, part_width], F32, name="sums") for part in parts]
+                for k in range(row_blocks):
+                    for bank, part in zip(sums, parts):
+                        nc.tensor.matmul(bank[:], weights[k][:, c::out_blocks],
+                                         x[k][:, start + part:start + part + part_width],
+                                         start=(k == 0), stop=(k == row_blocks - 1))
+                for bank, part in zip(sums, parts):
+                    part_result = result[:, part:part + part_width]
+                    if part == 0:
+                        nc.scalar.activation(part_result, bank[:], ACT.Relu, bias=bias[:, c:c + 1])
                     else:
-                        nc.scalar.activation(result[:, c - first, :], sums[c][:], ACT.Relu,
-                                             bias=bias[:, c:c + 1])
-                nc.sync.dma_start(out_by_block[:, first:first + PAIR, columns], result[:])
+                        nc.vector.tensor_scalar(part_result, bank[:], bias[:, c:c + 1], 0.0, ALU.add, ALU.max)
+                nc.sync.dma_start(out_by_block[:, c, start:start + width], result[:])
+            start += width

@@ -27,11 +27,6 @@ def tile_lookup_gnorm_relu_kernel(tc, tab, w, b, offs, out):
         tc.tile_pool(name="held", bufs=1) as held,
         tc.psum_pool(name="psum", bufs=BANKS) as psum,
     ):
-        warm_in = held.tile([P, 1], F32, name="warm_in")
-        warm_out = held.tile([P, 1], F32, name="warm_out")
-        nc.vector.memset(warm_in[:], 0.0)
-        nc.scalar.activation(warm_out[:], warm_in[:], ACT.Sigmoid)
-
         offsets = held.tile([P, n_total // GROUP], U16, name="offsets")
         bias = held.tile([P, out_blocks], F32, name="bias")
         nc.sync.dma_start(offsets[:], offs)

import concourse.mybir as mybir

F32, BF16, U16 = mybir.dt.float32, mybir.dt.bfloat16, mybir.dt.uint16
ALU = mybir.AluOpType
ACT = mybir.ActivationFunctionType

P = 128
GROUP = 16
PIECE = 256
BANK = 512
BANKS = 8
STORE_WIDTHS = (PIECE, PIECE, 4 * PIECE)
SHIFT, SCALE = 0.125, 1.5
FLOPS = 2 * 256 * 512 * 1536


def tile_lookup_gnorm_relu_kernel(tc, tab, w, b, offs, out):
    nc = tc.nc
    rows, places = tab.shape[1], tab.shape[2]
    m_total, n_total = out.shape
    row_blocks, out_blocks, pieces = rows // P, m_total // P, n_total // PIECE
    assert sum(STORE_WIDTHS) == n_total

    out_by_block = out.rearrange("(p c) n -> p c n", c=out_blocks)

    with (
        tc.tile_pool(name="held", bufs=1) as held,
        tc.psum_pool(name="psum", bufs=BANKS) as psum,
    ):
        offsets = held.tile([P, n_total // GROUP], U16, name="offsets")
        bias = held.tile([P, out_blocks], F32, name="bias")
        nc.sync.dma_start(offsets[:], offs)
        values, gates, weights = [], [], []
        for k in range(row_blocks):
            block_rows = slice(k * P, (k + 1) * P)
            gates.append(held.tile([P, places], F32, name=f"gates{k}"))
            values.append(held.tile([P, places], F32, name=f"values{k}"))
            weights.append(held.tile([P, m_total], BF16, name=f"weights{k}"))
            nc.sync.dma_start(gates[k][:], tab[1, block_rows, :])
            nc.sync.dma_start(values[k][:], tab[0, block_rows, :])
            nc.sync.dma_start(weights[k][:], w[block_rows, :])
        nc.sync.dma_start(bias[:], b.rearrange("(p c) o -> p (c o)", c=out_blocks))

        x = [held.tile([P, n_total], BF16, name=f"x{k}") for k in range(row_blocks)]
        for k in range(row_blocks):
            for step in range(pieces):
                j = (step + pieces // 2) % pieces if k == 0 else step
                listed = offsets[:, j * PIECE // GROUP:(j + 1) * PIECE // GROUP]
                gate = held.tile([P, PIECE], F32, name=f"gate{k}_{j}")
                normed = held.tile([P, PIECE], F32, name=f"normed{k}_{j}")
                nc.scalar.activation(gate[:], gates[k][:].indirect(listed), ACT.Sigmoid)
                nc.vector.tensor_scalar(normed[:], values[k][:].indirect(listed), SHIFT, SCALE,
                                        ALU.subtract, ALU.mult)
                late = k == row_blocks - 1 and step >= pieces - 2
                multiplier = nc.vector if late else nc.gpsimd
                multiplier.tensor_tensor(x[k][:, j * PIECE:(j + 1) * PIECE], normed[:], gate[:], ALU.mult)

        start = 0
        for width in STORE_WIDTHS:
            for c in range(out_blocks):
                result = held.tile([P, width], F32, name=f"result{start}_{c}")
                part_width = min(width, BANK)
                parts = range(0, width, part_width)
                sums = [psum.tile([P, part_width], F32, name="sums") for part in parts]
                for k in range(row_blocks):
                    for bank, part in zip(sums, parts):
                        nc.tensor.matmul(bank[:], weights[k][:, c::out_blocks],
                                         x[k][:, start + part:start + part + part_width],
                                         start=(k == 0), stop=(k == row_blocks - 1))
                for bank, part in zip(sums, parts):
                    part_result = result[:, part:part + part_width]
                    if part == 0:
                        nc.scalar.activation(part_result, bank[:], ACT.Relu, bias=bias[:, c:c + 1])
                    else:
                        nc.vector.tensor_scalar(part_result, bank[:], bias[:, c:c + 1], 0.0, ALU.add, ALU.max)
                nc.sync.dma_start(out_by_block[:, c, start:start + width], result[:])
            start += width
